import numpy as np
import ml_dtypes


def mxq(x, axis, fmt="e4m3"):
    dtype, down = {"e4m3": (ml_dtypes.float8_e4m3fn, 7), "e5m2": (ml_dtypes.float8_e5m2, 14)}[fmt]
    v = np.moveaxis(np.asarray(x, np.float32).astype(ml_dtypes.bfloat16).astype(np.float64), axis, -1)
    blocks = v.reshape(v.shape[:-1] + (-1, 32))
    amax = np.abs(blocks).max(-1, keepdims=True)
    byte = np.maximum(np.where(amax > 0, np.frexp(amax)[1] - 1 + 127, 0) - down, 1)
    scale = np.exp2(byte - 127.0)
    codes = (blocks / scale).astype(np.float32).astype(dtype).astype(np.float64)
    return np.moveaxis((codes * scale).reshape(v.shape), -1, axis)


WIDE = False


def mx_kscale(k):
    if not WIDE:
        return np.ones(k)
    levels = np.array([10, -10, 5, -5, 0])
    if k % 512:
        return np.exp2(np.random.permutation(np.resize(levels, k // 32))).repeat(32)
    a = np.empty((k // 512, 16))
    for p in range(k // 512):
        a[p, :8] = np.random.permutation(np.resize(levels, 8))
        for g in range(8):
            far = levels[np.abs(levels - a[p, g]) >= 10]
            a[p, g + 8] = far[np.random.randint(len(far))]
    return np.exp2(a.ravel()).repeat(32)


def f64(x):
    return np.asarray(x).astype(np.float64)


def striped(idx):
    return np.tile(idx.reshape(-1, 16).T, (8, 1)).astype(np.uint16)


def unstriped(offs):
    return offs[:16].T.reshape(-1).astype(np.int64)


def pack_weight(w):
    k, n = w.shape
    w = f64(np.asarray(w, np.float32).astype(ml_dtypes.bfloat16)).reshape(k // 32, 32, n)
    amax = np.abs(w).max(1)
    byte = np.clip(np.where(amax > 0, np.frexp(amax)[1] - 1 + 127 - 7, 1), 1, 254)
    scaled = (w * np.exp2(127.0 - byte)[:, None, :]).reshape(k, n).astype(np.float32)
    words = np.ascontiguousarray(scaled.reshape(k // 512, 128, 4, n).transpose(0, 1, 3, 2)).astype(ml_dtypes.float8_e4m3fn).view(np.uint8)
    return words, np.ascontiguousarray(byte.astype(np.uint8).reshape(k // 512, 16, n))


def unpack_weight(words, scales):
    g, p, n, _ = words.shape
    vals = np.ascontiguousarray(words).view(ml_dtypes.float8_e4m3fn).astype(np.float64) * np.repeat(np.exp2(scales.astype(np.float64) - 127.0), 8, axis=1)[..., None]
    return vals.transpose(0, 1, 3, 2).reshape(g * 512, n)


def planes(y):
    n, m = y.shape
    v = y.astype(np.float32).astype(ml_dtypes.bfloat16).astype(np.float64).reshape(n // 32, 32, m)
    top = np.abs(v).max(1)
    byte = np.clip(np.where(top > 0, np.frexp(top)[1] - 1 + 127 - 7, 1), 1, 254)
    codes = (v * np.exp2(127.0 - byte)[:, None, :]).reshape(n, m).astype(np.float32).astype(ml_dtypes.float8_e4m3fn).view(np.uint8)
    words = codes.reshape(n // 512, 128, 4, m).transpose(0, 1, 3, 2)
    return np.ascontiguousarray(words), np.ascontiguousarray(byte.astype(np.uint8).reshape(n // 512, 16, m))


K, T, S, N, H, W, U = 512, 2048, 512, 512, 512, 1024, 1024


def setup_inputs():
    n = np.random.standard_normal
    s = mx_kscale(K)[:, None]
    u = mx_kscale(H)
    packed_xT = pack_weight(n((K, T)) * s)
    packed_eT = pack_weight(n((K, W)) * s)
    return {
        "x_words": packed_xT[0],
        "x_scales": packed_xT[1],
        "w1": (n((K, N)) / np.sqrt(K) / s).astype(np.float32),
        "e_words": packed_eT[0],
        "e_scales": packed_eT[1],
        "w2": (n((K, N)) / np.sqrt(K) / s).astype(np.float32),
        "unit": (np.random.uniform(0.6, 1.4, (H, 1)) * u[:, None]).astype(np.float32),
        "w3": (n((H, N)) / np.sqrt(H) / u[:, None]).astype(np.float32),
        "offs": striped(np.random.permutation(T)[:S]),
        "drv": striped(np.random.permutation(W)[:S]),
        "r1": striped(np.random.permutation(np.concatenate([np.arange(S), np.random.randint(0, S, U - S)]))),
        "r2": striped(np.random.permutation(np.concatenate([np.arange(S), np.random.randint(0, S, U - S)]))),
        "d1": striped(np.random.permutation(np.concatenate([np.arange(S), np.random.randint(0, S, U - S)]))),
        "d2": striped(np.random.permutation(np.concatenate([np.arange(S), np.random.randint(0, S, U - S)]))),
    }


def reference(x_words, x_scales, w1, e_words, e_scales, w2, unit, w3, offs, drv, r1, r2, d1, d2):
    xq = unpack_weight(x_words, x_scales)[:, unstriped(offs)]
    y = mxq(f64(w1), 0, "e4m3").T @ xq
    y_1 = y[:, unstriped(r1)]
    y_2 = y[:, unstriped(r2)]
    e_drv = unpack_weight(e_words, e_scales)[:, unstriped(drv)]
    ye = mxq(f64(w2), 0, "e4m3").T @ e_drv
    e_1 = ye[:, unstriped(d1)]
    shr = np.maximum(y_1, y_2) - e_1
    e_2 = ye[:, unstriped(d2)]
    hid = f64(unit) * (shr * e_2)
    out_0 = mxq(f64(w3), 0, "e4m3").T @ mxq(hid, 0, "e4m3")
    return (out_0,) + planes(out_0)

@@ -1,0 +1,244 @@
+from contextlib import ExitStack
+
+import concourse.mybir as mybir
+
+K, T, W, S, U = 512, 2048, 1024, 512, 1024
+FLOPS = 2 * K * 512 * S * 2 + 2 * 512 * 512 * U
+
+F32 = mybir.dt.float32
+BF16 = mybir.dt.bfloat16
+I32 = mybir.dt.int32
+U32 = mybir.dt.uint32
+U16 = mybir.dt.uint16
+U8 = mybir.dt.uint8
+FP8X4 = mybir.dt.float8_e4m3fn_x4
+ALU = mybir.AluOpType
+COPY = mybir.ActivationFunctionType.Copy
+
+P = 128
+PACK = 4
+HALF = 256
+CHUNKS = (256, 256, 256, 128, 128)
+HID_ON_SCALAR = ()
+OUT_ON_VECTOR = (4,)
+
+
+def tile_picked_yroutef_max_po_kernel(
+    tc, x_words, x_scales, w1, e_words, e_scales, w2, unit, w3, offs, drv, r1, r2, d1, d2, out_0, out_1, out_2
+):
+    nc = tc.nc
+    with ExitStack() as ctx:
+        keep = ctx.enter_context(tc.tile_pool(name="keep", bufs=1))
+        ring = ctx.enter_context(tc.tile_pool(name="ring", bufs=2))
+        psum = ctx.enter_context(tc.psum_pool(name="psum", bufs=8))
+
+        def load_list(src, name):
+            tile = keep.tile(list(src.shape), U16, name=name)
+            nc.sync.dma_start(tile[:], src)
+            return tile
+
+        def load_weight(w, lo, hi, name):
+            raw = keep.tile([P, PACK, hi - lo], F32, name=name)
+            nc.sync.dma_start(raw[:], w.rearrange("(p j) c -> p j c", j=PACK)[:, :, lo:hi])
+            return raw
+
+        def load_words(src, cols, name):
+            tile = keep.tile([P, cols], I32, name=name)
+            nc.sync.dma_start(tile[:], src[0].rearrange("p c r -> p (c r)").bitcast(I32))
+            return tile
+
+        def load_scales(src, tile):
+            for q in range(4):
+                nc.sync.dma_start(tile[32 * q : 32 * q + 4, :].bitcast(I32), src[0][4 * q : 4 * q + 4, :].bitcast(I32))
+
+        def round_weight_half(engine_copy, raw_half, h, grouped):
+            dst = grouped[:].rearrange("p t m j -> p m j t")[:, h * (HALF // PACK) : (h + 1) * (HALF // PACK), :, :]
+            engine_copy(dst, raw_half.rearrange("p j (m t) -> p m j t", t=PACK))
+
+        def quantise_weight(grouped, name):
+            codes = keep.tile([P, 512], U32, name=name + "_codes", align_bytes=64)
+            scales = keep.tile([P, 512], U8, name=name + "_scales", align_bytes=64)
+            nc.vector.quantize_mx(
+                out=codes[:].bitcast(FP8X4), scales=scales[:], in_=grouped[:].rearrange("p t m j -> p (t m j)")
+            )
+            return codes, scales
+
+        def product(out, w_mx, t, codes, scales):
+            cols = slice(t * P, (t + 1) * P)
+            nc.tensor.matmul_mx(
+                out=out,
+                lhsT=w_mx[0][:, cols].bitcast(FP8X4),
+                lhsT_scale=w_mx[1][:, cols],
+                rhs=codes.bitcast(FP8X4),
+                rhs_scale=scales,
+                start=True,
+                stop=True,
+            )
+
+        def interleave(engine_copy, dst, src):
+            engine_copy(
+                dst[:].rearrange("p (c i) t -> p c t i", i=4), src[:].rearrange("p t (c i) -> p c t i", i=4)
+            )
+
+        xs_table = keep.tile([P, T], U8, name="xs_table")
+        es_table = keep.tile([P, W], U8, name="es_table")
+        nc.vector.memset(xs_table[:].bitcast(I32), 0)
+        nc.vector.memset(es_table[:].bitcast(I32), 0)
+        w1_raw = load_weight(w1, 0, 512, "w1_raw")
+        load_scales(x_scales, xs_table)
+        xw_table = load_words(x_words, T, "xw_table")
+        offs_sb = load_list(offs, "offs_sb")
+        drv_sb = load_list(drv, "drv_sb")
+        w2_raw = [load_weight(w2, 0, HALF, "w2_raw0")]
+        load_scales(e_scales, es_table)
+        w2_raw.append(load_weight(w2, HALF, 512, "w2_raw1"))
+        r1_sb = load_list(r1, "r1_sb")
+        r2_sb = load_list(r2, "r2_sb")
+        ew_table = load_words(e_words, W, "ew_table")
+        unit_sb = keep.tile([P, PACK], F32, name="unit_sb")
+        nc.sync.dma_start(unit_sb[:], unit.rearrange("(p t) o -> p (t o)", t=PACK))
+        d1_sb = load_list(d1, "d1_sb")
+        d2_sb = load_list(d2, "d2_sb")
+        w3_raw = [load_weight(w3, h * HALF, (h + 1) * HALF, "w3_raw%d" % h) for h in range(2)]
+
+        w1_bf = keep.tile([P, PACK, P, PACK], BF16, name="w1_bf", align_bytes=64)
+        round_weight_half(nc.scalar.copy, w1_raw[:, :, 0:HALF], 0, w1_bf)
+        round_weight_half(nc.vector.tensor_copy, w1_raw[:, :, HALF:512], 1, w1_bf)
+        xs = keep.tile([P, S], U8, name="xs", align_bytes=64)
+        nc.vector.tensor_copy(xs[:], xs_table[:].indirect(offs_sb[:]))
+        w1_mx = quantise_weight(w1_bf, "w1")
+        xw = keep.tile([P, S], U32, name="xw", align_bytes=64)
+        nc.vector.tensor_copy(xw[:], xw_table[:].bitcast(U32).indirect(offs_sb[:]))
+        y_acc = []
+        for t in range(PACK):
+            acc = psum.tile([P, S], F32, name="acc")
+            product(acc[:], w1_mx, t, xw[:], xs[:])
+            y_acc.append(acc)
+
+        es = keep.tile([P, S], U8, name="es", align_bytes=64)
+        nc.vector.tensor_copy(es[:], es_table[:].indirect(drv_sb[:]))
+        w2_bf = keep.tile([P, PACK, P, PACK], BF16, name="w2_bf", align_bytes=64)
+        round_weight_half(nc.scalar.copy, w2_raw[0][:], 0, w2_bf)
+        round_weight_half(nc.vector.tensor_copy, w2_raw[1][:], 1, w2_bf)
+        ew = keep.tile([P, S], U32, name="ew", align_bytes=64)
+        nc.vector.tensor_copy(ew[:], ew_table[:].bitcast(U32).indirect(drv_sb[:]))
+        w2_mx = quantise_weight(w2_bf, "w2")
+        ye_acc = []
+        for t in range(PACK):
+            acc = psum.tile([P, S], F32, name="acc")
+            product(acc[:], w2_mx, t, ew[:], es[:])
+            ye_acc.append(acc)
+
+        y = [keep.tile([P, S], F32, name="y%d" % t) for t in range(PACK)]
+        ye_neg = [keep.tile([P, S], F32, name="ye_neg%d" % t) for t in range(PACK)]
+        ye_unit = [keep.tile([P, S], F32, name="ye_unit%d" % t) for t in range(PACK)]
+
+        out_rows = out_0.rearrange("(p t) r -> p t r", t=PACK)
+        out_words = out_1[0].rearrange("p c r -> p (c r)").bitcast(I32)
+        o_codes = keep.tile([P, U], U32, name="o_codes", align_bytes=64)
+        o_scales = keep.tile([P, U], U8, name="o_scales", align_bytes=64)
+        w3_bf = keep.tile([P, PACK, P, PACK], BF16, name="w3_bf", align_bytes=64)
+        w3_mx = []
+
+        starts = [sum(CHUNKS[:c]) for c in range(len(CHUNKS))]
+        steps = [(c, pair) for c in range(len(CHUNKS)) for pair in range(2)]
+        larger, hid, hid_bf, h_mx, res_bf = {}, {}, {}, {}, {}
+
+        def entries(c):
+            return slice(starts[c] // 16, (starts[c] + CHUNKS[c]) // 16)
+
+        def fetch_requests(step):
+            c, pair = step
+            y_1 = ring.tile([P, 2, CHUNKS[c]], F32, name="y_1")
+            y_2 = ring.tile([P, 2, CHUNKS[c]], F32, name="y_2")
+            for i in range(2):
+                t = 2 * pair + i
+                if c == 0:
+                    nc.scalar.copy(y[t][:], y_acc[t][:])
+                nc.scalar.activation(y_1[:, i, :], y[t][:].indirect(r1_sb[:, entries(c)]), COPY)
+                nc.scalar.activation(y_2[:, i, :], y[t][:].indirect(r2_sb[:, entries(c)]), COPY)
+            return y_1, y_2
+
+        def take_larger(step, y_1, y_2):
+            larger[step] = ring.tile([P, 2, CHUNKS[step[0]]], F32, name="larger")
+            nc.vector.tensor_tensor(larger[step][:], y_1[:], y_2[:], ALU.max)
+
+        def round_hidden(c):
+            hid_bf[c] = ring.tile([P, CHUNKS[c], PACK], BF16, name="hid_bf", align_bytes=64)
+            interleave(nc.scalar.copy if c in HID_ON_SCALAR else nc.vector.tensor_copy, hid_bf[c], hid[c])
+
+        def quantise_hidden(c):
+            codes = ring.tile([P, CHUNKS[c]], U32, name="h_codes", align_bytes=64)
+            scales = ring.tile([P, CHUNKS[c]], U8, name="h_scales", align_bytes=64)
+            nc.vector.quantize_mx(
+                out=codes[:].bitcast(FP8X4), scales=scales[:], in_=hid_bf[c][:].rearrange("p r t -> p (r t)")
+            )
+            h_mx[c] = (codes, scales)
+
+        def last_product(c):
+            n = CHUNKS[c]
+            res = ring.tile([P, PACK, n], F32, name="res")
+            per_bank = 512 // n
+            for first in range(0, PACK, per_bank):
+                acc = psum.tile([P, per_bank, n], F32, name="acc")
+                for i in range(per_bank):
+                    product(acc[:, i, :], w3_mx, first + i, h_mx[c][0][:], h_mx[c][1][:])
+                nc.scalar.copy(res[:, first : first + per_bank, :], acc[:])
+            nc.sync.dma_start(out_rows[:, :, starts[c] : starts[c] + n], res[:])
+            res_bf[c] = ring.tile([P, n, PACK], BF16, name="res_bf", align_bytes=64)
+            interleave(nc.vector.tensor_copy if c in OUT_ON_VECTOR else nc.scalar.copy, res_bf[c], res)
+
+        def quantise_result(c):
+            cols = slice(starts[c], starts[c] + CHUNKS[c])
+            nc.vector.quantize_mx(
+                out=o_codes[:, cols].bitcast(FP8X4),
+                scales=o_scales[:, cols],
+                in_=res_bf[c][:].rearrange("p r t -> p (r t)"),
+            )
+            nc.sync.dma_start(out_words[:, cols], o_codes[:, cols].bitcast(I32))
+
+        first_pair = fetch_requests(steps[0])
+        take_larger(steps[0], first_pair[0], first_pair[1])
+        for n, step in enumerate(steps):
+            c, pair = step
+            if pair == 0:
+                hid[c] = ring.tile([P, PACK, CHUNKS[c]], F32, name="hid")
+            if n + 1 < len(steps):
+                ahead = fetch_requests(steps[n + 1])
+            if n == 1:
+                for h in range(2):
+                    round_weight_half(nc.scalar.copy, w3_raw[h][:], h, w3_bf)
+            shr = ring.tile([P, 2, CHUNKS[c]], F32, name="shr")
+            if c == 0:
+                for i in range(2):
+                    t = 2 * pair + i
+                    nc.vector.tensor_scalar(ye_neg[t][:], ye_acc[t][:], -1.0, None, ALU.mult)
+                for i in range(2):
+                    t = 2 * pair + i
+                    nc.vector.tensor_scalar(ye_unit[t][:], ye_neg[t][:], unit_sb[:, t : t + 1], -1.0, ALU.mult, ALU.mult)
+            for i in range(2):
+                window = ye_neg[2 * pair + i][:].indirect(d1_sb[:, entries(c)])
+                nc.vector.tensor_tensor(shr[:, i, :], window, larger[step][:, i, :], ALU.add)
+            if n + 1 < len(steps):
+                take_larger(steps[n + 1], ahead[0], ahead[1])
+            if pair == 0 and c > 0:
+                round_hidden(c - 1)
+            if n == 2:
+                w3_mx.extend(quantise_weight(w3_bf, "w3"))
+            for i in range(2):
+                window = ye_unit[2 * pair + i][:].indirect(d2_sb[:, entries(c)])
+                nc.vector.tensor_tensor(hid[c][:, 2 * pair + i, :], window, shr[:, i, :], ALU.mult)
+            if pair == 0 and c > 0:
+                quantise_hidden(c - 1)
+                last_product(c - 1)
+            if pair == 0 and c > 1:
+                quantise_result(c - 2)
+        last = len(CHUNKS) - 1
+        round_hidden(last)
+        quantise_result(last - 1)
+        quantise_hidden(last)
+        last_product(last)
+        quantise_result(last)
+        for q in range(4):
+            queue = nc.sync if q % 2 == 0 else nc.scalar
+            queue.dma_start(out_2[0][4 * q : 4 * q + 4, :].bitcast(I32), o_scales[32 * q : 32 * q + 4, :].bitcast(I32))

@@ -18,9 +18,12 @@ COPY = mybir.ActivationFunctionType.Copy
 P = 128
 PACK = 4
 HALF = 256
-CHUNKS = (256, 256, 256, 128, 128)
-HID_ON_SCALAR = ()
-OUT_ON_VECTOR = (4,)
+CHUNKS = (512, 256, 256)
+SPARE = 16
+PIECES = (256, 256, 256, 128, 128)
+FUSED = 512
+OUT_ON_SCALAR = (512,)
+GROUP = 2
 
 
 def tile_picked_yroutef_max_po_kernel(
@@ -47,9 +50,12 @@ def tile_picked_yroutef_max_po_kernel(
             nc.sync.dma_start(tile[:], src[0].rearrange("p c r -> p (c r)").bitcast(I32))
             return tile
 
-        def load_scales(src, tile):
-            for q in range(4):
-                nc.sync.dma_start(tile[32 * q : 32 * q + 4, :].bitcast(I32), src[0][4 * q : 4 * q + 4, :].bitcast(I32))
+        def load_scales(queues, src, cols, name):
+            tile = keep.tile([P, cols], U8, name=name)
+            for q, queue in enumerate(queues):
+                rows = src[0][4 * q : 4 * q + 4, :].bitcast(I32)
+                queue.dma_start(tile[32 * q : 32 * q + 32, :].bitcast(I32), rows.unsqueeze(0).to_broadcast([8, 4, cols // 4]))
+            return tile
 
         def round_weight_half(engine_copy, raw_half, h, grouped):
             dst = grouped[:].rearrange("p t m j -> p m j t")[:, h * (HALF // PACK) : (h + 1) * (HALF // PACK), :, :]
@@ -77,29 +83,26 @@ def tile_picked_yroutef_max_po_kernel(
 
         def interleave(engine_copy, dst, src):
             engine_copy(
-                dst[:].rearrange("p (c i) t -> p c t i", i=4), src[:].rearrange("p t (c i) -> p c t i", i=4)
+                dst.rearrange("p (c i) t -> p c t i", i=4), src.rearrange("p t (c i) -> p c t i", i=4)
             )
 
-        xs_table = keep.tile([P, T], U8, name="xs_table")
-        es_table = keep.tile([P, W], U8, name="es_table")
-        nc.vector.memset(xs_table[:].bitcast(I32), 0)
-        nc.vector.memset(es_table[:].bitcast(I32), 0)
         w1_raw = load_weight(w1, 0, 512, "w1_raw")
-        load_scales(x_scales, xs_table)
-        xw_table = load_words(x_words, T, "xw_table")
+        xs_table = load_scales([nc.sync] * 4, x_scales, T, "xs_table")
         offs_sb = load_list(offs, "offs_sb")
+        xw_table = load_words(x_words, T, "xw_table")
+        w2_lo = load_weight(w2, 0, HALF, "w2_raw0")
+        es_table = load_scales([nc.gpsimd, nc.gpsimd, nc.sync, nc.sync], e_scales, W, "es_table")
         drv_sb = load_list(drv, "drv_sb")
-        w2_raw = [load_weight(w2, 0, HALF, "w2_raw0")]
-        load_scales(e_scales, es_table)
-        w2_raw.append(load_weight(w2, HALF, 512, "w2_raw1"))
         r1_sb = load_list(r1, "r1_sb")
         r2_sb = load_list(r2, "r2_sb")
+        w2_hi = load_weight(w2, HALF, 512, "w2_raw1")
         ew_table = load_words(e_words, W, "ew_table")
-        unit_sb = keep.tile([P, PACK], F32, name="unit_sb")
-        nc.sync.dma_start(unit_sb[:], unit.rearrange("(p t) o -> p (t o)", t=PACK))
         d1_sb = load_list(d1, "d1_sb")
         d2_sb = load_list(d2, "d2_sb")
         w3_raw = [load_weight(w3, h * HALF, (h + 1) * HALF, "w3_raw%d" % h) for h in range(2)]
+        unit_sb = keep.tile([P, PACK], F32, name="unit_sb")
+        nc.gpsimd.dma_start(unit_sb[:], unit.rearrange("(p t) o -> p (t o)", t=PACK))
+        w2_raw = [w2_lo, w2_hi]
 
         w1_bf = keep.tile([P, PACK, P, PACK], BF16, name="w1_bf", align_bytes=64)
         round_weight_half(nc.scalar.copy, w1_raw[:, :, 0:HALF], 0, w1_bf)
@@ -129,9 +132,11 @@ def tile_picked_yroutef_max_po_kernel(
             product(acc[:], w2_mx, t, ew[:], es[:])
             ye_acc.append(acc)
 
-        y = [keep.tile([P, S], F32, name="y%d" % t) for t in range(PACK)]
-        ye_neg = [keep.tile([P, S], F32, name="ye_neg%d" % t) for t in range(PACK)]
-        ye_unit = [keep.tile([P, S], F32, name="ye_unit%d" % t) for t in range(PACK)]
+        y = [keep.tile([P, S + SPARE], F32, name="y%d" % t) for t in range(PACK)]
+        ye_neg = [keep.tile([P, S + SPARE], F32, name="ye_neg%d" % t) for t in range(PACK)]
+        ye_unit = [keep.tile([P, S + SPARE], F32, name="ye_unit%d" % t) for t in range(PACK)]
+        for window in y + ye_neg + ye_unit:
+            nc.vector.memset(window[:, S:], 0.0)
 
         out_rows = out_0.rearrange("(p t) r -> p t r", t=PACK)
         out_words = out_1[0].rearrange("p c r -> p (c r)").bitcast(I32)
@@ -141,104 +146,123 @@ def tile_picked_yroutef_max_po_kernel(
         w3_mx = []
 
         starts = [sum(CHUNKS[:c]) for c in range(len(CHUNKS))]
-        steps = [(c, pair) for c in range(len(CHUNKS)) for pair in range(2)]
-        larger, hid, hid_bf, h_mx, res_bf = {}, {}, {}, {}, {}
+        steps = [(c, first) for c in range(len(CHUNKS)) for first in range(0, PACK, GROUP)]
+        pieces = [(sum(PIECES[:k]), PIECES[k]) for k in range(len(PIECES))]
+        larger = {}
+        shr = [keep.tile([P, PACK, n], F32, name="shr%d" % c) for c, n in enumerate(CHUNKS)]
+        other = [keep.tile([P, PACK, n], F32, name="other%d" % c) for c, n in enumerate(CHUNKS)]
+        res = {lo: keep.tile([P, PACK, n], F32, name="res%d" % lo) for lo, n in pieces}
+        hid_bf = {lo: keep.tile([P, n, PACK], BF16, name="hid_bf%d" % lo, align_bytes=64) for lo, n in pieces}
+        res_bf = {lo: keep.tile([P, n, PACK], BF16, name="res_bf%d" % lo, align_bytes=64) for lo, n in pieces}
 
-        def entries(c):
-            return slice(starts[c] // 16, (starts[c] + CHUNKS[c]) // 16)
+        def entries(lo, hi):
+            return slice(lo // 16, hi // 16)
 
         def fetch_requests(step):
-            c, pair = step
-            y_1 = ring.tile([P, 2, CHUNKS[c]], F32, name="y_1")
-            y_2 = ring.tile([P, 2, CHUNKS[c]], F32, name="y_2")
-            for i in range(2):
-                t = 2 * pair + i
+            c, first = step
+            e = entries(starts[c], starts[c] + CHUNKS[c])
+            y_1 = ring.tile([P, GROUP, CHUNKS[c]], F32, name="y_1", bufs=2)
+            y_2 = ring.tile([P, GROUP, CHUNKS[c]], F32, name="y_2", bufs=2)
+            for i in range(GROUP):
+                t = first + i
                 if c == 0:
-                    nc.scalar.copy(y[t][:], y_acc[t][:])
-                nc.scalar.activation(y_1[:, i, :], y[t][:].indirect(r1_sb[:, entries(c)]), COPY)
-                nc.scalar.activation(y_2[:, i, :], y[t][:].indirect(r2_sb[:, entries(c)]), COPY)
+                    nc.scalar.copy(y[t][:, :S], y_acc[t][:])
+                nc.scalar.activation(y_1[:, i, :], y[t][:].indirect(r1_sb[:, e]), COPY)
+                nc.scalar.activation(y_2[:, i, :], y[t][:].indirect(r2_sb[:, e]), COPY)
             return y_1, y_2
 
         def take_larger(step, y_1, y_2):
-            larger[step] = ring.tile([P, 2, CHUNKS[step[0]]], F32, name="larger")
+            larger[step] = ring.tile([P, GROUP, CHUNKS[step[0]]], F32, name="larger", bufs=2)
             nc.vector.tensor_tensor(larger[step][:], y_1[:], y_2[:], ALU.max)
 
-        def round_hidden(c):
-            hid_bf[c] = ring.tile([P, CHUNKS[c], PACK], BF16, name="hid_bf", align_bytes=64)
-            interleave(nc.scalar.copy if c in HID_ON_SCALAR else nc.vector.tensor_copy, hid_bf[c], hid[c])
+        def round_hidden(c, lo, n):
+            cols = slice(lo - starts[c], lo - starts[c] + n)
+            if lo < FUSED:
+                interleave(nc.vector.tensor_copy, hid_bf[lo][:], other[c][:, :, cols])
+            else:
+                nc.vector.tensor_tensor(
+                    hid_bf[lo][:].rearrange("p (c i) t -> p c t i", i=2),
+                    shr[c][:, :, cols].rearrange("p t (c i) -> p c t i", i=2),
+                    other[c][:, :, cols].rearrange("p t (c i) -> p c t i", i=2),
+                    ALU.mult,
+                )
 
-        def quantise_hidden(c):
-            codes = ring.tile([P, CHUNKS[c]], U32, name="h_codes", align_bytes=64)
-            scales = ring.tile([P, CHUNKS[c]], U8, name="h_scales", align_bytes=64)
+        def last_product(c, lo, n):
+            cols = slice(lo, lo + n)
+            h_codes = keep.tile([P, n], U32, name="h_codes%d" % lo, align_bytes=64)
+            h_scales = keep.tile([P, n], U8, name="h_scales%d" % lo, align_bytes=64)
             nc.vector.quantize_mx(
-                out=codes[:].bitcast(FP8X4), scales=scales[:], in_=hid_bf[c][:].rearrange("p r t -> p (r t)")
+                out=h_codes[:].bitcast(FP8X4),
+                scales=h_scales[:],
+                in_=hid_bf[lo][:].rearrange("p r t -> p (r t)"),
             )
-            h_mx[c] = (codes, scales)
-
-        def last_product(c):
-            n = CHUNKS[c]
-            res = ring.tile([P, PACK, n], F32, name="res")
             per_bank = 512 // n
             for first in range(0, PACK, per_bank):
                 acc = psum.tile([P, per_bank, n], F32, name="acc")
                 for i in range(per_bank):
-                    product(acc[:, i, :], w3_mx, first + i, h_mx[c][0][:], h_mx[c][1][:])
-                nc.scalar.copy(res[:, first : first + per_bank, :], acc[:])
-            nc.sync.dma_start(out_rows[:, :, starts[c] : starts[c] + n], res[:])
-            res_bf[c] = ring.tile([P, n, PACK], BF16, name="res_bf", align_bytes=64)
-            interleave(nc.vector.tensor_copy if c in OUT_ON_VECTOR else nc.scalar.copy, res_bf[c], res)
+                    product(acc[:, i, :], w3_mx, first + i, h_codes[:], h_scales[:])
+                nc.scalar.copy(res[lo][:, first : first + per_bank, :], acc[:])
+            nc.sync.dma_start(out_rows[:, :, cols], res[lo][:])
 
-        def quantise_result(c):
-            cols = slice(starts[c], starts[c] + CHUNKS[c])
+        def round_result(c, lo, n):
+            interleave(nc.scalar.copy if lo in OUT_ON_SCALAR else nc.vector.tensor_copy, res_bf[lo][:], res[lo][:])
+
+        def quantise_result(c, lo, n):
+            cols = slice(lo, lo + n)
             nc.vector.quantize_mx(
                 out=o_codes[:, cols].bitcast(FP8X4),
                 scales=o_scales[:, cols],
-                in_=res_bf[c][:].rearrange("p r t -> p (r t)"),
+                in_=res_bf[lo][:].rearrange("p r t -> p (r t)"),
             )
             nc.sync.dma_start(out_words[:, cols], o_codes[:, cols].bitcast(I32))
 
-        first_pair = fetch_requests(steps[0])
-        take_larger(steps[0], first_pair[0], first_pair[1])
+        def finish(c, stage):
+            for lo, n in pieces:
+                if starts[c] <= lo < starts[c] + CHUNKS[c]:
+                    stage(c, lo, n)
+
+        ahead = fetch_requests(steps[0])
+        take_larger(steps[0], ahead[0], ahead[1])
         for n, step in enumerate(steps):
-            c, pair = step
-            if pair == 0:
-                hid[c] = ring.tile([P, PACK, CHUNKS[c]], F32, name="hid")
+            c, first = step
+            lo, hi = starts[c], starts[c] + CHUNKS[c]
+            split = min(max(FUSED, lo), hi)
+            group = range(first, first + GROUP)
             if n + 1 < len(steps):
                 ahead = fetch_requests(steps[n + 1])
             if n == 1:
                 for h in range(2):
                     round_weight_half(nc.scalar.copy, w3_raw[h][:], h, w3_bf)
-            shr = ring.tile([P, 2, CHUNKS[c]], F32, name="shr")
             if c == 0:
-                for i in range(2):
-                    t = 2 * pair + i
-                    nc.vector.tensor_scalar(ye_neg[t][:], ye_acc[t][:], -1.0, None, ALU.mult)
-                for i in range(2):
-                    t = 2 * pair + i
-                    nc.vector.tensor_scalar(ye_unit[t][:], ye_neg[t][:], unit_sb[:, t : t + 1], -1.0, ALU.mult, ALU.mult)
-            for i in range(2):
-                window = ye_neg[2 * pair + i][:].indirect(d1_sb[:, entries(c)])
-                nc.vector.tensor_tensor(shr[:, i, :], window, larger[step][:, i, :], ALU.add)
+                for t in group:
+                    nc.vector.tensor_scalar(ye_neg[t][:, :S], ye_acc[t][:], -1.0, None, ALU.mult)
+                for t in group:
+                    nc.vector.tensor_scalar(ye_unit[t][:, :S], ye_neg[t][:, :S], unit_sb[:, t : t + 1], -1.0, ALU.mult, ALU.mult)
+            if split < hi:
+                for t in group:
+                    nc.scalar.activation(other[c][:, t, split - lo :], ye_unit[t][:].indirect(d2_sb[:, entries(split, hi)]), COPY)
+            for t in group:
+                window = ye_neg[t][:].indirect(d1_sb[:, entries(lo, hi)])
+                nc.vector.tensor_tensor(shr[c][:, t, :], window, larger[step][:, t - first, :], ALU.add)
             if n + 1 < len(steps):
                 take_larger(steps[n + 1], ahead[0], ahead[1])
-            if pair == 0 and c > 0:
-                round_hidden(c - 1)
-            if n == 2:
+            if first == 0 and c > 0:
+                finish(c - 1, round_hidden)
+            if first == 0 and c == 1:
                 w3_mx.extend(quantise_weight(w3_bf, "w3"))
-            for i in range(2):
-                window = ye_unit[2 * pair + i][:].indirect(d2_sb[:, entries(c)])
-                nc.vector.tensor_tensor(hid[c][:, 2 * pair + i, :], window, shr[:, i, :], ALU.mult)
-            if pair == 0 and c > 0:
-                quantise_hidden(c - 1)
-                last_product(c - 1)
-            if pair == 0 and c > 1:
-                quantise_result(c - 2)
+            if first == PACK - GROUP and c > 0 and GROUP < PACK:
+                finish(c - 1, round_result)
+            if lo < split:
+                for t in group:
+                    window = ye_unit[t][:].indirect(d2_sb[:, entries(lo, split)])
+                    nc.vector.tensor_tensor(other[c][:, t, : split - lo], window, shr[c][:, t, : split - lo], ALU.mult)
+            if first == 0 and c > 0:
+                finish(c - 1, last_product)
+            if first == PACK - GROUP and c > 0:
+                finish(c - 1, quantise_result)
         last = len(CHUNKS) - 1
-        round_hidden(last)
-        quantise_result(last - 1)
-        quantise_hidden(last)
-        last_product(last)
-        quantise_result(last)
+        for stage in (round_hidden, last_product, round_result, quantise_result):
+            finish(last, stage)
         for q in range(4):
             queue = nc.sync if q % 2 == 0 else nc.scalar
             queue.dma_start(out_2[0][4 * q : 4 * q + 4, :].bitcast(I32), o_scales[32 * q : 32 * q + 4, :].bitcast(I32))

@@ -2,8 +2,11 @@ from contextlib import ExitStack
 
 import concourse.mybir as mybir
 
-K, T, W, S, U = 512, 2048, 1024, 512, 1024
-FLOPS = 2 * K * 512 * S * 2 + 2 * 512 * 512 * U
+K = 512
+T, W = 2048, 1024
+S = 512
+U = 1024
+FLOPS = 2 * K * K * (2 * S + U)
 
 F32 = mybir.dt.float32
 BF16 = mybir.dt.bfloat16
@@ -16,14 +19,18 @@ ALU = mybir.AluOpType
 COPY = mybir.ActivationFunctionType.Copy
 
 P = 128
-PACK = 4
-HALF = 256
-CHUNKS = (512, 256, 256)
+SLOTS = 4
+QUADRANTS = 4
+BANK = 512
+HALF = K // 2
+LIST_GROUP = 16
 SPARE = 16
-PIECES = (256, 256, 256, 128, 128)
-FUSED = 512
-OUT_ON_SCALAR = (512,)
-GROUP = 2
+
+CHUNKS = (128, 512, 256, 128)
+LONG = CHUNKS.index(max(CHUNKS))
+FUSED_CHUNKS = LONG + 1
+PIECE = 256
+REQUEST_BUFS = 5
 
 
 def tile_picked_yroutef_max_po_kernel(
@@ -33,6 +40,7 @@ def tile_picked_yroutef_max_po_kernel(
     with ExitStack() as ctx:
         keep = ctx.enter_context(tc.tile_pool(name="keep", bufs=1))
         ring = ctx.enter_context(tc.tile_pool(name="ring", bufs=2))
+        reused = ctx.enter_context(tc.tile_pool(name="reused", bufs=1))
         psum = ctx.enter_context(tc.psum_pool(name="psum", bufs=8))
 
         def load_list(src, name):
@@ -41,8 +49,8 @@ def tile_picked_yroutef_max_po_kernel(
             return tile
 
         def load_weight(w, lo, hi, name):
-            raw = keep.tile([P, PACK, hi - lo], F32, name=name)
-            nc.sync.dma_start(raw[:], w.rearrange("(p j) c -> p j c", j=PACK)[:, :, lo:hi])
+            raw = keep.tile([P, SLOTS, hi - lo], F32, name=name)
+            nc.sync.dma_start(raw[:], w.rearrange("(p j) c -> p j c", j=SLOTS)[:, :, lo:hi])
             return raw
 
         def load_words(src, cols, name):
@@ -50,23 +58,24 @@ def tile_picked_yroutef_max_po_kernel(
             nc.sync.dma_start(tile[:], src[0].rearrange("p c r -> p (c r)").bitcast(I32))
             return tile
 
-        def load_scales(queues, src, cols, name):
-            tile = keep.tile([P, cols], U8, name=name)
-            for q, queue in enumerate(queues):
-                rows = src[0][4 * q : 4 * q + 4, :].bitcast(I32)
-                queue.dma_start(tile[32 * q : 32 * q + 32, :].bitcast(I32), rows.unsqueeze(0).to_broadcast([8, 4, cols // 4]))
-            return tile
+        def load_scales(src, tile):
+            for q in range(QUADRANTS):
+                nc.sync.dma_start(tile[32 * q : 32 * q + 4, :].bitcast(I32), src[0][4 * q : 4 * q + 4, :].bitcast(I32))
 
-        def round_weight_half(engine_copy, raw_half, h, grouped):
-            dst = grouped[:].rearrange("p t m j -> p m j t")[:, h * (HALF // PACK) : (h + 1) * (HALF // PACK), :, :]
-            engine_copy(dst, raw_half.rearrange("p j (m t) -> p m j t", t=PACK))
+        def round_weight_half(engine_copy, raw_half, h, dealt):
+            dst = dealt[:].rearrange("p t m j -> p m j t")[:, h * (HALF // SLOTS) : (h + 1) * (HALF // SLOTS), :, :]
+            engine_copy(dst, raw_half.rearrange("p j (m t) -> p m j t", t=SLOTS))
 
-        def quantise_weight(grouped, name):
-            codes = keep.tile([P, 512], U32, name=name + "_codes", align_bytes=64)
-            scales = keep.tile([P, 512], U8, name=name + "_scales", align_bytes=64)
-            nc.vector.quantize_mx(
-                out=codes[:].bitcast(FP8X4), scales=scales[:], in_=grouped[:].rearrange("p t m j -> p (t m j)")
-            )
+        def quantise(codes, scales, rounded):
+            nc.vector.quantize_mx(out=codes.bitcast(FP8X4), scales=scales, in_=rounded)
+
+        def quantise_weight(dealt, codes, scales):
+            quantise(codes[:], scales[:], dealt[:].rearrange("p t m j -> p (t m j)"))
+            return codes, scales
+
+        def weight_mx_tiles(name):
+            codes = keep.tile([P, K], U32, name=name + "_codes", align_bytes=64)
+            scales = keep.tile([P, K], U8, name=name + "_scales", align_bytes=64)
             return codes, scales
 
         def product(out, w_mx, t, codes, scales):
@@ -81,188 +90,203 @@ def tile_picked_yroutef_max_po_kernel(
                 stop=True,
             )
 
-        def interleave(engine_copy, dst, src):
-            engine_copy(
-                dst.rearrange("p (c i) t -> p c t i", i=4), src.rearrange("p t (c i) -> p c t i", i=4)
-            )
+        def as_words(ap):
+            return ap.rearrange("p (c i) t -> p c t i", i=4)
 
-        w1_raw = load_weight(w1, 0, 512, "w1_raw")
-        xs_table = load_scales([nc.sync] * 4, x_scales, T, "xs_table")
+        def as_slots(ap):
+            return ap.rearrange("p t (c i) -> p c t i", i=4)
+
+        xs_table = keep.tile([P, T], U8, name="xs_table")
+        es_table = keep.tile([P, W], U8, name="es_table")
+        nc.vector.memset(xs_table[:].bitcast(I32), 0)
+        nc.vector.memset(es_table[:].bitcast(I32), 0)
         offs_sb = load_list(offs, "offs_sb")
-        xw_table = load_words(x_words, T, "xw_table")
-        w2_lo = load_weight(w2, 0, HALF, "w2_raw0")
-        es_table = load_scales([nc.gpsimd, nc.gpsimd, nc.sync, nc.sync], e_scales, W, "es_table")
         drv_sb = load_list(drv, "drv_sb")
         r1_sb = load_list(r1, "r1_sb")
         r2_sb = load_list(r2, "r2_sb")
-        w2_hi = load_weight(w2, HALF, 512, "w2_raw1")
-        ew_table = load_words(e_words, W, "ew_table")
         d1_sb = load_list(d1, "d1_sb")
         d2_sb = load_list(d2, "d2_sb")
-        w3_raw = [load_weight(w3, h * HALF, (h + 1) * HALF, "w3_raw%d" % h) for h in range(2)]
-        unit_sb = keep.tile([P, PACK], F32, name="unit_sb")
-        nc.gpsimd.dma_start(unit_sb[:], unit.rearrange("(p t) o -> p (t o)", t=PACK))
-        w2_raw = [w2_lo, w2_hi]
+        unit_sb = keep.tile([P, SLOTS], F32, name="unit_sb")
+        nc.sync.dma_start(unit_sb[:], unit.rearrange("(p t) o -> p (t o)", t=SLOTS))
+        w1_raw = load_weight(w1, 0, K, "w1_raw")
+        load_scales(x_scales, xs_table)
+        xw_table = load_words(x_words, T, "xw_table")
+        w2_low = load_weight(w2, 0, HALF, "w2_low")
+        load_scales(e_scales, es_table)
+        ew_table = load_words(e_words, W, "ew_table")
+        w2_high = load_weight(w2, HALF, K, "w2_high")
+        w3_low = load_weight(w3, 0, HALF, "w3_low")
+        w3_high = load_weight(w3, HALF, K, "w3_high")
 
-        w1_bf = keep.tile([P, PACK, P, PACK], BF16, name="w1_bf", align_bytes=64)
-        round_weight_half(nc.scalar.copy, w1_raw[:, :, 0:HALF], 0, w1_bf)
-        round_weight_half(nc.vector.tensor_copy, w1_raw[:, :, HALF:512], 1, w1_bf)
+        w1_bf = keep.tile([P, SLOTS, P, SLOTS], BF16, name="w1_bf", align_bytes=64)
+        round_weight_half(nc.scalar.copy, w1_raw[:, :, :HALF], 0, w1_bf)
+        round_weight_half(nc.vector.tensor_copy, w1_raw[:, :, HALF:], 1, w1_bf)
         xs = keep.tile([P, S], U8, name="xs", align_bytes=64)
         nc.vector.tensor_copy(xs[:], xs_table[:].indirect(offs_sb[:]))
-        w1_mx = quantise_weight(w1_bf, "w1")
+        w1_mx = quantise_weight(w1_bf, *weight_mx_tiles("w1"))
         xw = keep.tile([P, S], U32, name="xw", align_bytes=64)
         nc.vector.tensor_copy(xw[:], xw_table[:].bitcast(U32).indirect(offs_sb[:]))
         y_acc = []
-        for t in range(PACK):
+        for t in range(SLOTS):
             acc = psum.tile([P, S], F32, name="acc")
             product(acc[:], w1_mx, t, xw[:], xs[:])
             y_acc.append(acc)
 
+        larger_bytes = K * 4
         es = keep.tile([P, S], U8, name="es", align_bytes=64)
         nc.vector.tensor_copy(es[:], es_table[:].indirect(drv_sb[:]))
-        w2_bf = keep.tile([P, PACK, P, PACK], BF16, name="w2_bf", align_bytes=64)
-        round_weight_half(nc.scalar.copy, w2_raw[0][:], 0, w2_bf)
-        round_weight_half(nc.vector.tensor_copy, w2_raw[1][:], 1, w2_bf)
         ew = keep.tile([P, S], U32, name="ew", align_bytes=64)
         nc.vector.tensor_copy(ew[:], ew_table[:].bitcast(U32).indirect(drv_sb[:]))
-        w2_mx = quantise_weight(w2_bf, "w2")
+        w2_bf = keep.tile([P, SLOTS, P, SLOTS], BF16, name="w2_bf", align_bytes=64)
+        round_weight_half(nc.scalar.copy, w2_low[:], 0, w2_bf)
+        round_weight_half(nc.vector.tensor_copy, w2_high[:], 1, w2_bf)
+        w2_codes = reused.tile([P, K], U32, name="w2_codes", align_bytes=64, offset=0)
+        w2_scales = reused.tile([P, K], U8, name="w2_scales", align_bytes=64, offset=larger_bytes)
+        w2_mx = quantise_weight(w2_bf, w2_codes, w2_scales)
         ye_acc = []
-        for t in range(PACK):
+        for t in range(SLOTS):
             acc = psum.tile([P, S], F32, name="acc")
             product(acc[:], w2_mx, t, ew[:], es[:])
             ye_acc.append(acc)
 
-        y = [keep.tile([P, S + SPARE], F32, name="y%d" % t) for t in range(PACK)]
-        ye_neg = [keep.tile([P, S + SPARE], F32, name="ye_neg%d" % t) for t in range(PACK)]
-        ye_unit = [keep.tile([P, S + SPARE], F32, name="ye_unit%d" % t) for t in range(PACK)]
+        y = [keep.tile([P, S + SPARE], F32, name="y%d" % t) for t in range(SLOTS)]
+        ye_neg = [keep.tile([P, S + SPARE], F32, name="ye_neg%d" % t) for t in range(SLOTS)]
+        ye_unit = [keep.tile([P, S + SPARE], F32, name="ye_unit%d" % t) for t in range(SLOTS)]
         for window in y + ye_neg + ye_unit:
             nc.vector.memset(window[:, S:], 0.0)
 
-        out_rows = out_0.rearrange("(p t) r -> p t r", t=PACK)
+        out_rows = out_0.rearrange("(p t) r -> p t r", t=SLOTS)
         out_words = out_1[0].rearrange("p c r -> p (c r)").bitcast(I32)
-        o_codes = keep.tile([P, U], U32, name="o_codes", align_bytes=64)
-        o_scales = keep.tile([P, U], U8, name="o_scales", align_bytes=64)
-        w3_bf = keep.tile([P, PACK, P, PACK], BF16, name="w3_bf", align_bytes=64)
-        w3_mx = []
+        out_codes = keep.tile([P, U], U32, name="out_codes", align_bytes=64)
+        out_scales = keep.tile([P, U], U8, name="out_scales", align_bytes=64)
+        w3_bf = keep.tile([P, SLOTS, P, SLOTS], BF16, name="w3_bf", align_bytes=64)
+        w3_mx = weight_mx_tiles("w3")
 
+        last = len(CHUNKS) - 1
         starts = [sum(CHUNKS[:c]) for c in range(len(CHUNKS))]
-        steps = [(c, first) for c in range(len(CHUNKS)) for first in range(0, PACK, GROUP)]
-        pieces = [(sum(PIECES[:k]), PIECES[k]) for k in range(len(PIECES))]
-        larger = {}
-        shr = [keep.tile([P, PACK, n], F32, name="shr%d" % c) for c, n in enumerate(CHUNKS)]
-        other = [keep.tile([P, PACK, n], F32, name="other%d" % c) for c, n in enumerate(CHUNKS)]
-        res = {lo: keep.tile([P, PACK, n], F32, name="res%d" % lo) for lo, n in pieces}
-        hid_bf = {lo: keep.tile([P, n, PACK], BF16, name="hid_bf%d" % lo, align_bytes=64) for lo, n in pieces}
-        res_bf = {lo: keep.tile([P, n, PACK], BF16, name="res_bf%d" % lo, align_bytes=64) for lo, n in pieces}
+        step_slots = [1 if c < FUSED_CHUNKS else 2 for c in range(len(CHUNKS))]
+        steps = [(c, first) for c in range(len(CHUNKS)) for first in range(0, SLOTS, step_slots[c])]
+        pieces = [
+            [(lo, min(PIECE, CHUNKS[c])) for lo in range(starts[c], starts[c] + CHUNKS[c], PIECE)]
+            for c in range(len(CHUNKS))
+        ]
+        all_pieces = [piece for of_chunk in pieces for piece in of_chunk]
+        long_end = starts[LONG] + CHUNKS[LONG]
+        word_stores = {long_end: 0, U: long_end}
 
-        def entries(lo, hi):
-            return slice(lo // 16, hi // 16)
+        larger = {}
+        shr = [keep.tile([P, SLOTS, n], F32, name="shr%d" % c) for c, n in enumerate(CHUNKS)]
+        second = {}
+        res = {lo: keep.tile([P, SLOTS, n], F32, name="res%d" % lo) for lo, n in all_pieces}
+        hid_bf = {lo: keep.tile([P, n, SLOTS], BF16, name="hid_bf%d" % lo, align_bytes=64) for lo, n in all_pieces}
+        res_bf = {lo: keep.tile([P, n, SLOTS], BF16, name="res_bf%d" % lo, align_bytes=64) for lo, n in all_pieces}
+
+        def entries(list_sb, c):
+            return list_sb[:, starts[c] // LIST_GROUP : (starts[c] + CHUNKS[c]) // LIST_GROUP]
 
         def fetch_requests(step):
             c, first = step
-            e = entries(starts[c], starts[c] + CHUNKS[c])
-            y_1 = ring.tile([P, GROUP, CHUNKS[c]], F32, name="y_1", bufs=2)
-            y_2 = ring.tile([P, GROUP, CHUNKS[c]], F32, name="y_2", bufs=2)
-            for i in range(GROUP):
+            y_1 = ring.tile([P, step_slots[c], CHUNKS[c]], F32, name="y_1", bufs=REQUEST_BUFS)
+            y_2 = ring.tile([P, step_slots[c], CHUNKS[c]], F32, name="y_2", bufs=REQUEST_BUFS)
+            for i in range(step_slots[c]):
                 t = first + i
                 if c == 0:
                     nc.scalar.copy(y[t][:, :S], y_acc[t][:])
-                nc.scalar.activation(y_1[:, i, :], y[t][:].indirect(r1_sb[:, e]), COPY)
-                nc.scalar.activation(y_2[:, i, :], y[t][:].indirect(r2_sb[:, e]), COPY)
+                nc.scalar.activation(y_1[:, i, :], y[t][:].indirect(entries(r1_sb, c)), COPY)
+                nc.scalar.activation(y_2[:, i, :], y[t][:].indirect(entries(r2_sb, c)), COPY)
             return y_1, y_2
 
         def take_larger(step, y_1, y_2):
-            larger[step] = ring.tile([P, GROUP, CHUNKS[step[0]]], F32, name="larger", bufs=2)
+            c = step[0]
+            larger[step] = reused.tile(
+                [P, step_slots[c], CHUNKS[c]], F32, name="larger", bufs=2, align_bytes=64, offset=0
+            )
             nc.vector.tensor_tensor(larger[step][:], y_1[:], y_2[:], ALU.max)
 
         def round_hidden(c, lo, n):
             cols = slice(lo - starts[c], lo - starts[c] + n)
-            if lo < FUSED:
-                interleave(nc.vector.tensor_copy, hid_bf[lo][:], other[c][:, :, cols])
+            if c < FUSED_CHUNKS:
+                nc.vector.tensor_copy(as_words(hid_bf[lo][:]), as_slots(second[c][:, :, cols]))
             else:
                 nc.vector.tensor_tensor(
-                    hid_bf[lo][:].rearrange("p (c i) t -> p c t i", i=2),
-                    shr[c][:, :, cols].rearrange("p t (c i) -> p c t i", i=2),
-                    other[c][:, :, cols].rearrange("p t (c i) -> p c t i", i=2),
-                    ALU.mult,
+                    as_words(hid_bf[lo][:]), as_slots(shr[c][:, :, cols]), as_slots(second[c][:, :, cols]), ALU.mult
                 )
 
         def last_product(c, lo, n):
-            cols = slice(lo, lo + n)
             h_codes = keep.tile([P, n], U32, name="h_codes%d" % lo, align_bytes=64)
             h_scales = keep.tile([P, n], U8, name="h_scales%d" % lo, align_bytes=64)
-            nc.vector.quantize_mx(
-                out=h_codes[:].bitcast(FP8X4),
-                scales=h_scales[:],
-                in_=hid_bf[lo][:].rearrange("p r t -> p (r t)"),
-            )
-            per_bank = 512 // n
-            for first in range(0, PACK, per_bank):
+            quantise(h_codes[:], h_scales[:], hid_bf[lo][:].rearrange("p r t -> p (r t)"))
+            per_bank = BANK // n
+            for first in range(0, SLOTS, per_bank):
                 acc = psum.tile([P, per_bank, n], F32, name="acc")
                 for i in range(per_bank):
                     product(acc[:, i, :], w3_mx, first + i, h_codes[:], h_scales[:])
                 nc.scalar.copy(res[lo][:, first : first + per_bank, :], acc[:])
-            nc.sync.dma_start(out_rows[:, :, cols], res[lo][:])
+            nc.sync.dma_start(out_rows[:, :, lo : lo + n], res[lo][:])
 
         def round_result(c, lo, n):
-            interleave(nc.scalar.copy if lo in OUT_ON_SCALAR else nc.vector.tensor_copy, res_bf[lo][:], res[lo][:])
+            engine_copy = nc.scalar.copy if c == LONG else nc.vector.tensor_copy
+            engine_copy(as_words(res_bf[lo][:]), as_slots(res[lo][:]))
 
         def quantise_result(c, lo, n):
-            cols = slice(lo, lo + n)
-            nc.vector.quantize_mx(
-                out=o_codes[:, cols].bitcast(FP8X4),
-                scales=o_scales[:, cols],
-                in_=res_bf[lo][:].rearrange("p r t -> p (r t)"),
-            )
-            nc.sync.dma_start(out_words[:, cols], o_codes[:, cols].bitcast(I32))
+            end = lo + n
+            quantise(out_codes[:, lo:end], out_scales[:, lo:end], res_bf[lo][:].rearrange("p r t -> p (r t)"))
+            if end in word_stores:
+                done = slice(word_stores[end], end)
+                nc.sync.dma_start(out_words[:, done], out_codes[:, done].bitcast(I32))
 
-        def finish(c, stage):
-            for lo, n in pieces:
-                if starts[c] <= lo < starts[c] + CHUNKS[c]:
-                    stage(c, lo, n)
+        def for_pieces(c, stage):
+            for lo, n in pieces[c]:
+                stage(c, lo, n)
 
-        ahead = fetch_requests(steps[0])
-        take_larger(steps[0], ahead[0], ahead[1])
+        take_larger(steps[0], *fetch_requests(steps[0]))
         for n, step in enumerate(steps):
             c, first = step
-            lo, hi = starts[c], starts[c] + CHUNKS[c]
-            split = min(max(FUSED, lo), hi)
-            group = range(first, first + GROUP)
-            if n + 1 < len(steps):
-                ahead = fetch_requests(steps[n + 1])
+            slots = range(first, first + step_slots[c])
+            opens_chunk = first == 0
+            has_next = n + 1 < len(steps)
+            if opens_chunk:
+                second[c] = ring.tile([P, SLOTS, CHUNKS[c]], F32, name="second")
+            if has_next:
+                requests = fetch_requests(steps[n + 1])
             if n == 1:
-                for h in range(2):
-                    round_weight_half(nc.scalar.copy, w3_raw[h][:], h, w3_bf)
+                round_weight_half(nc.vector.tensor_copy, w3_low[:], 0, w3_bf)
+                round_weight_half(nc.scalar.copy, w3_high[:], 1, w3_bf)
             if c == 0:
-                for t in group:
+                for t in slots:
                     nc.vector.tensor_scalar(ye_neg[t][:, :S], ye_acc[t][:], -1.0, None, ALU.mult)
-                for t in group:
-                    nc.vector.tensor_scalar(ye_unit[t][:, :S], ye_neg[t][:, :S], unit_sb[:, t : t + 1], -1.0, ALU.mult, ALU.mult)
-            if split < hi:
-                for t in group:
-                    nc.scalar.activation(other[c][:, t, split - lo :], ye_unit[t][:].indirect(d2_sb[:, entries(split, hi)]), COPY)
-            for t in group:
-                window = ye_neg[t][:].indirect(d1_sb[:, entries(lo, hi)])
-                nc.vector.tensor_tensor(shr[c][:, t, :], window, larger[step][:, t - first, :], ALU.add)
-            if n + 1 < len(steps):
-                take_larger(steps[n + 1], ahead[0], ahead[1])
-            if first == 0 and c > 0:
-                finish(c - 1, round_hidden)
-            if first == 0 and c == 1:
-                w3_mx.extend(quantise_weight(w3_bf, "w3"))
-            if first == PACK - GROUP and c > 0 and GROUP < PACK:
-                finish(c - 1, round_result)
-            if lo < split:
-                for t in group:
-                    window = ye_unit[t][:].indirect(d2_sb[:, entries(lo, split)])
-                    nc.vector.tensor_tensor(other[c][:, t, : split - lo], window, shr[c][:, t, : split - lo], ALU.mult)
-            if first == 0 and c > 0:
-                finish(c - 1, last_product)
-            if first == PACK - GROUP and c > 0:
-                finish(c - 1, quantise_result)
-        last = len(CHUNKS) - 1
-        for stage in (round_hidden, last_product, round_result, quantise_result):
-            finish(last, stage)
-        for q in range(4):
+                    nc.vector.tensor_scalar(
+                        ye_unit[t][:, :S], ye_neg[t][:, :S], unit_sb[:, t : t + 1], -1.0, ALU.mult, ALU.mult
+                    )
+            if c >= FUSED_CHUNKS:
+                for t in slots:
+                    nc.scalar.activation(second[c][:, t, :], ye_unit[t][:].indirect(entries(d2_sb, c)), COPY)
+            for t in slots:
+                first_driver = ye_neg[t][:].indirect(entries(d1_sb, c))
+                nc.vector.tensor_tensor(shr[c][:, t, :], first_driver, larger[step][:, t - first, :], ALU.add)
+            if has_next:
+                take_larger(steps[n + 1], *requests)
+            if opens_chunk and c >= 1:
+                for_pieces(c - 1, round_hidden)
+            if opens_chunk and c == 1:
+                quantise_weight(w3_bf, *w3_mx)
+            if opens_chunk and c >= 2:
+                for_pieces(c - 2, round_result)
+            if c < FUSED_CHUNKS:
+                for t in slots:
+                    second_driver = ye_unit[t][:].indirect(entries(d2_sb, c))
+                    nc.vector.tensor_tensor(second[c][:, t, :], second_driver, shr[c][:, t, :], ALU.mult)
+            if opens_chunk and c >= 1:
+                for_pieces(c - 1, last_product)
+            if opens_chunk and c >= 2:
+                for_pieces(c - 2, quantise_result)
+        for_pieces(last, round_hidden)
+        for_pieces(last - 1, round_result)
+        for_pieces(last, last_product)
+        for_pieces(last - 1, quantise_result)
+        for_pieces(last, round_result)
+        for_pieces(last, quantise_result)
+
+        for q in range(QUADRANTS):
             queue = nc.sync if q % 2 == 0 else nc.scalar
-            queue.dma_start(out_2[0][4 * q : 4 * q + 4, :].bitcast(I32), o_scales[32 * q : 32 * q + 4, :].bitcast(I32))
+            queue.dma_start(out_2[0][4 * q : 4 * q + 4, :].bitcast(I32), out_scales[32 * q : 32 * q + 4, :].bitcast(I32))

from contextlib import ExitStack

import concourse.mybir as mybir

K = 512
T, W = 2048, 1024
S = 512
U = 1024
FLOPS = 2 * K * K * (2 * S + U)

F32 = mybir.dt.float32
BF16 = mybir.dt.bfloat16
I32 = mybir.dt.int32
U32 = mybir.dt.uint32
U16 = mybir.dt.uint16
U8 = mybir.dt.uint8
FP8X4 = mybir.dt.float8_e4m3fn_x4
ALU = mybir.AluOpType
COPY = mybir.ActivationFunctionType.Copy

P = 128
SLOTS = 4
QUADRANTS = 4
BANK = 512
HALF = K // 2
LIST_GROUP = 16
SPARE = 16

CHUNKS = (128, 512, 256, 128)
LONG = CHUNKS.index(max(CHUNKS))
FUSED_CHUNKS = LONG + 1
PIECE = 256
REQUEST_BUFS = 5


def tile_picked_yroutef_max_po_kernel(
    tc, x_words, x_scales, w1, e_words, e_scales, w2, unit, w3, offs, drv, r1, r2, d1, d2, out_0, out_1, out_2
):
    nc = tc.nc
    with ExitStack() as ctx:
        keep = ctx.enter_context(tc.tile_pool(name="keep", bufs=1))
        ring = ctx.enter_context(tc.tile_pool(name="ring", bufs=2))
        reused = ctx.enter_context(tc.tile_pool(name="reused", bufs=1))
        psum = ctx.enter_context(tc.psum_pool(name="psum", bufs=8))

        def load_list(src, name):
            tile = keep.tile(list(src.shape), U16, name=name)
            nc.sync.dma_start(tile[:], src)
            return tile

        def load_weight(w, lo, hi, name):
            raw = keep.tile([P, SLOTS, hi - lo], F32, name=name)
            nc.sync.dma_start(raw[:], w.rearrange("(p j) c -> p j c", j=SLOTS)[:, :, lo:hi])
            return raw

        def load_words(src, cols, name):
            tile = keep.tile([P, cols], I32, name=name)
            nc.sync.dma_start(tile[:], src[0].rearrange("p c r -> p (c r)").bitcast(I32))
            return tile

        def load_scales(src, tile):
            for q in range(QUADRANTS):
                nc.sync.dma_start(tile[32 * q : 32 * q + 4, :].bitcast(I32), src[0][4 * q : 4 * q + 4, :].bitcast(I32))

        def round_weight_half(engine_copy, raw_half, h, dealt):
            dst = dealt[:].rearrange("p t m j -> p m j t")[:, h * (HALF // SLOTS) : (h + 1) * (HALF // SLOTS), :, :]
            engine_copy(dst, raw_half.rearrange("p j (m t) -> p m j t", t=SLOTS))

        def quantise(codes, scales, rounded):
            nc.vector.quantize_mx(out=codes.bitcast(FP8X4), scales=scales, in_=rounded)

        def quantise_weight(dealt, codes, scales):
            quantise(codes[:], scales[:], dealt[:].rearrange("p t m j -> p (t m j)"))
            return codes, scales

        def weight_mx_tiles(name):
            codes = keep.tile([P, K], U32, name=name + "_codes", align_bytes=64)
            scales = keep.tile([P, K], U8, name=name + "_scales", align_bytes=64)
            return codes, scales

        def product(out, w_mx, t, codes, scales):
            cols = slice(t * P, (t + 1) * P)
            nc.tensor.matmul_mx(
                out=out,
                lhsT=w_mx[0][:, cols].bitcast(FP8X4),
                lhsT_scale=w_mx[1][:, cols],
                rhs=codes.bitcast(FP8X4),
                rhs_scale=scales,
                start=True,
                stop=True,
            )

        def as_words(ap):
            return ap.rearrange("p (c i) t -> p c t i", i=4)

        def as_slots(ap):
            return ap.rearrange("p t (c i) -> p c t i", i=4)

        xs_table = keep.tile([P, T], U8, name="xs_table")
        es_table = keep.tile([P, W], U8, name="es_table")
        nc.vector.memset(xs_table[:].bitcast(I32), 0)
        nc.vector.memset(es_table[:].bitcast(I32), 0)
        offs_sb = load_list(offs, "offs_sb")
        drv_sb = load_list(drv, "drv_sb")
        r1_sb = load_list(r1, "r1_sb")
        r2_sb = load_list(r2, "r2_sb")
        d1_sb = load_list(d1, "d1_sb")
        d2_sb = load_list(d2, "d2_sb")
        unit_sb = keep.tile([P, SLOTS], F32, name="unit_sb")
        nc.sync.dma_start(unit_sb[:], unit.rearrange("(p t) o -> p (t o)", t=SLOTS))
        w1_raw = load_weight(w1, 0, K, "w1_raw")
        load_scales(x_scales, xs_table)
        xw_table = load_words(x_words, T, "xw_table")
        w2_low = load_weight(w2, 0, HALF, "w2_low")
        load_scales(e_scales, es_table)
        ew_table = load_words(e_words, W, "ew_table")
        w2_high = load_weight(w2, HALF, K, "w2_high")
        w3_low = load_weight(w3, 0, HALF, "w3_low")
        w3_high = load_weight(w3, HALF, K, "w3_high")

        w1_bf = keep.tile([P, SLOTS, P, SLOTS], BF16, name="w1_bf", align_bytes=64)
        round_weight_half(nc.scalar.copy, w1_raw[:, :, :HALF], 0, w1_bf)
        round_weight_half(nc.vector.tensor_copy, w1_raw[:, :, HALF:], 1, w1_bf)
        xs = keep.tile([P, S], U8, name="xs", align_bytes=64)
        nc.vector.tensor_copy(xs[:], xs_table[:].indirect(offs_sb[:]))
        w1_mx = quantise_weight(w1_bf, *weight_mx_tiles("w1"))
        xw = keep.tile([P, S], U32, name="xw", align_bytes=64)
        nc.vector.tensor_copy(xw[:], xw_table[:].bitcast(U32).indirect(offs_sb[:]))
        y_acc = []
        for t in range(SLOTS):
            acc = psum.tile([P, S], F32, name="acc")
            product(acc[:], w1_mx, t, xw[:], xs[:])
            y_acc.append(acc)

        larger_bytes = K * 4
        es = keep.tile([P, S], U8, name="es", align_bytes=64)
        nc.vector.tensor_copy(es[:], es_table[:].indirect(drv_sb[:]))
        ew = keep.tile([P, S], U32, name="ew", align_bytes=64)
        nc.vector.tensor_copy(ew[:], ew_table[:].bitcast(U32).indirect(drv_sb[:]))
        w2_bf = keep.tile([P, SLOTS, P, SLOTS], BF16, name="w2_bf", align_bytes=64)
        round_weight_half(nc.scalar.copy, w2_low[:], 0, w2_bf)
        round_weight_half(nc.vector.tensor_copy, w2_high[:], 1, w2_bf)
        w2_codes = reused.tile([P, K], U32, name="w2_codes", align_bytes=64, offset=0)
        w2_scales = reused.tile([P, K], U8, name="w2_scales", align_bytes=64, offset=larger_bytes)
        w2_mx = quantise_weight(w2_bf, w2_codes, w2_scales)
        ye_acc = []
        for t in range(SLOTS):
            acc = psum.tile([P, S], F32, name="acc")
            product(acc[:], w2_mx, t, ew[:], es[:])
            ye_acc.append(acc)

        y = [keep.tile([P, S + SPARE], F32, name="y%d" % t) for t in range(SLOTS)]
        ye_neg = [keep.tile([P, S + SPARE], F32, name="ye_neg%d" % t) for t in range(SLOTS)]
        ye_unit = [keep.tile([P, S + SPARE], F32, name="ye_unit%d" % t) for t in range(SLOTS)]
        for window in y + ye_neg + ye_unit:
            nc.vector.memset(window[:, S:], 0.0)

        out_rows = out_0.rearrange("(p t) r -> p t r", t=SLOTS)
        out_words = out_1[0].rearrange("p c r -> p (c r)").bitcast(I32)
        out_codes = keep.tile([P, U], U32, name="out_codes", align_bytes=64)
        out_scales = keep.tile([P, U], U8, name="out_scales", align_bytes=64)
        w3_bf = keep.tile([P, SLOTS, P, SLOTS], BF16, name="w3_bf", align_bytes=64)
        w3_mx = weight_mx_tiles("w3")

        last = len(CHUNKS) - 1
        starts = [sum(CHUNKS[:c]) for c in range(len(CHUNKS))]
        step_slots = [1 if c < FUSED_CHUNKS else 2 for c in range(len(CHUNKS))]
        steps = [(c, first) for c in range(len(CHUNKS)) for first in range(0, SLOTS, step_slots[c])]
        pieces = [
            [(lo, min(PIECE, CHUNKS[c])) for lo in range(starts[c], starts[c] + CHUNKS[c], PIECE)]
            for c in range(len(CHUNKS))
        ]
        all_pieces = [piece for of_chunk in pieces for piece in of_chunk]
        long_end = starts[LONG] + CHUNKS[LONG]
        word_stores = {long_end: 0, U: long_end}

        larger = {}
        shr = [keep.tile([P, SLOTS, n], F32, name="shr%d" % c) for c, n in enumerate(CHUNKS)]
        second = {}
        res = {lo: keep.tile([P, SLOTS, n], F32, name="res%d" % lo) for lo, n in all_pieces}
        hid_bf = {lo: keep.tile([P, n, SLOTS], BF16, name="hid_bf%d" % lo, align_bytes=64) for lo, n in all_pieces}
        res_bf = {lo: keep.tile([P, n, SLOTS], BF16, name="res_bf%d" % lo, align_bytes=64) for lo, n in all_pieces}

        def entries(list_sb, c):
            return list_sb[:, starts[c] // LIST_GROUP : (starts[c] + CHUNKS[c]) // LIST_GROUP]

        def fetch_requests(step):
            c, first = step
            y_1 = ring.tile([P, step_slots[c], CHUNKS[c]], F32, name="y_1", bufs=REQUEST_BUFS)
            y_2 = ring.tile([P, step_slots[c], CHUNKS[c]], F32, name="y_2", bufs=REQUEST_BUFS)
            for i in range(step_slots[c]):
                t = first + i
                if c == 0:
                    nc.scalar.copy(y[t][:, :S], y_acc[t][:])
                nc.scalar.activation(y_1[:, i, :], y[t][:].indirect(entries(r1_sb, c)), COPY)
                nc.scalar.activation(y_2[:, i, :], y[t][:].indirect(entries(r2_sb, c)), COPY)
            return y_1, y_2

        def take_larger(step, y_1, y_2):
            c = step[0]
            larger[step] = reused.tile(
                [P, step_slots[c], CHUNKS[c]], F32, name="larger", bufs=2, align_bytes=64, offset=0
            )
            nc.vector.tensor_tensor(larger[step][:], y_1[:], y_2[:], ALU.max)

        def round_hidden(c, lo, n):
            cols = slice(lo - starts[c], lo - starts[c] + n)
            if c < FUSED_CHUNKS:
                nc.vector.tensor_copy(as_words(hid_bf[lo][:]), as_slots(second[c][:, :, cols]))
            else:
                nc.vector.tensor_tensor(
                    as_words(hid_bf[lo][:]), as_slots(shr[c][:, :, cols]), as_slots(second[c][:, :, cols]), ALU.mult
                )

        def last_product(c, lo, n):
            h_codes = keep.tile([P, n], U32, name="h_codes%d" % lo, align_bytes=64)
            h_scales = keep.tile([P, n], U8, name="h_scales%d" % lo, align_bytes=64)
            quantise(h_codes[:], h_scales[:], hid_bf[lo][:].rearrange("p r t -> p (r t)"))
            per_bank = BANK // n
            for first in range(0, SLOTS, per_bank):
                acc = psum.tile([P, per_bank, n], F32, name="acc")
                for i in range(per_bank):
                    product(acc[:, i, :], w3_mx, first + i, h_codes[:], h_scales[:])
                nc.scalar.copy(res[lo][:, first : first + per_bank, :], acc[:])
            nc.sync.dma_start(out_rows[:, :, lo : lo + n], res[lo][:])

        def round_result(c, lo, n):
            engine_copy = nc.scalar.copy if c == LONG else nc.vector.tensor_copy
            engine_copy(as_words(res_bf[lo][:]), as_slots(res[lo][:]))

        def quantise_result(c, lo, n):
            end = lo + n
            quantise(out_codes[:, lo:end], out_scales[:, lo:end], res_bf[lo][:].rearrange("p r t -> p (r t)"))
            if end in word_stores:
                done = slice(word_stores[end], end)
                nc.sync.dma_start(out_words[:, done], out_codes[:, done].bitcast(I32))

        def for_pieces(c, stage):
            for lo, n in pieces[c]:
                stage(c, lo, n)

        take_larger(steps[0], *fetch_requests(steps[0]))
        for n, step in enumerate(steps):
            c, first = step
            slots = range(first, first + step_slots[c])
            opens_chunk = first == 0
            has_next = n + 1 < len(steps)
            if opens_chunk:
                second[c] = ring.tile([P, SLOTS, CHUNKS[c]], F32, name="second")
            if has_next:
                requests = fetch_requests(steps[n + 1])
            if n == 1:
                round_weight_half(nc.vector.tensor_copy, w3_low[:], 0, w3_bf)
                round_weight_half(nc.scalar.copy, w3_high[:], 1, w3_bf)
            if c == 0:
                for t in slots:
                    nc.vector.tensor_scalar(ye_neg[t][:, :S], ye_acc[t][:], -1.0, None, ALU.mult)
                    nc.vector.tensor_scalar(
                        ye_unit[t][:, :S], ye_neg[t][:, :S], unit_sb[:, t : t + 1], -1.0, ALU.mult, ALU.mult
                    )
            if c >= FUSED_CHUNKS:
                for t in slots:
                    nc.scalar.activation(second[c][:, t, :], ye_unit[t][:].indirect(entries(d2_sb, c)), COPY)
            for t in slots:
                first_driver = ye_neg[t][:].indirect(entries(d1_sb, c))
                nc.vector.tensor_tensor(shr[c][:, t, :], first_driver, larger[step][:, t - first, :], ALU.add)
            if has_next:
                take_larger(steps[n + 1], *requests)
            if opens_chunk and c >= 1:
                for_pieces(c - 1, round_hidden)
            if opens_chunk and c == 1:
                quantise_weight(w3_bf, *w3_mx)
            if opens_chunk and c >= 2:
                for_pieces(c - 2, round_result)
            if c < FUSED_CHUNKS:
                for t in slots:
                    second_driver = ye_unit[t][:].indirect(entries(d2_sb, c))
                    nc.vector.tensor_tensor(second[c][:, t, :], second_driver, shr[c][:, t, :], ALU.mult)
            if opens_chunk and c >= 1:
                for_pieces(c - 1, last_product)
            if opens_chunk and c >= 2:
                for_pieces(c - 2, quantise_result)
        for_pieces(last, round_hidden)
        for_pieces(last - 1, round_result)
        for_pieces(last, last_product)
        for_pieces(last - 1, quantise_result)
        for_pieces(last, round_result)
        for_pieces(last, quantise_result)

        for q in range(QUADRANTS):
            queue = nc.sync if q % 2 == 0 else nc.scalar
            queue.dma_start(out_2[0][4 * q : 4 * q + 4, :].bitcast(I32), out_scales[32 * q : 32 * q + 4, :].bitcast(I32))
